import numpy as np
import ml_dtypes


def mxq(x, axis, fmt="e4m3"):
    dtype, down = {"e4m3": (ml_dtypes.float8_e4m3fn, 7), "e5m2": (ml_dtypes.float8_e5m2, 14)}[fmt]
    v = np.moveaxis(np.asarray(x, np.float32).astype(ml_dtypes.bfloat16).astype(np.float64), axis, -1)
    blocks = v.reshape(v.shape[:-1] + (-1, 32))
    amax = np.abs(blocks).max(-1, keepdims=True)
    byte = np.maximum(np.where(amax > 0, np.frexp(amax)[1] - 1 + 127, 0) - down, 1)
    scale = np.exp2(byte - 127.0)
    codes = (blocks / scale).astype(np.float32).astype(dtype).astype(np.float64)
    return np.moveaxis((codes * scale).reshape(v.shape), -1, axis)


WIDE = False


def mx_kscale(k):
    if not WIDE:
        return np.ones(k)
    levels = np.array([10, -10, 5, -5, 0])
    if k % 512:
        return np.exp2(np.random.permutation(np.resize(levels, k // 32))).repeat(32)
    a = np.empty((k // 512, 16))
    for p in range(k // 512):
        a[p, :8] = np.random.permutation(np.resize(levels, 8))
        for g in range(8):
            far = levels[np.abs(levels - a[p, g]) >= 10]
            a[p, g + 8] = far[np.random.randint(len(far))]
    return np.exp2(a.ravel()).repeat(32)


def f64(x):
    return np.asarray(x).astype(np.float64)


def striped(idx):
    return np.tile(idx.reshape(-1, 16).T, (8, 1)).astype(np.uint16)


def unstriped(offs):
    return offs[:16].T.reshape(-1).astype(np.int64)


def pack_weight(w):
    k, n = w.shape
    w = f64(np.asarray(w, np.float32).astype(ml_dtypes.bfloat16)).reshape(k // 32, 32, n)
    amax = np.abs(w).max(1)
    byte = np.clip(np.where(amax > 0, np.frexp(amax)[1] - 1 + 127 - 7, 1), 1, 254)
    scaled = (w * np.exp2(127.0 - byte)[:, None, :]).reshape(k, n).astype(np.float32)
    words = np.ascontiguousarray(scaled.reshape(k // 512, 128, 4, n).transpose(0, 1, 3, 2)).astype(ml_dtypes.float8_e4m3fn).view(np.uint8)
    return words, np.ascontiguousarray(byte.astype(np.uint8).reshape(k // 512, 16, n))


def unpack_weight(words, scales):
    g, p, n, _ = words.shape
    vals = np.ascontiguousarray(words).view(ml_dtypes.float8_e4m3fn).astype(np.float64) * np.repeat(np.exp2(scales.astype(np.float64) - 127.0), 8, axis=1)[..., None]
    return vals.transpose(0, 1, 3, 2).reshape(g * 512, n)


K, T, S, V, D, G = 1024, 1024, 512, 512, 8, 64
P = 2 ** 7


def setup_inputs():
    n = np.random.standard_normal
    s = mx_kscale(K)[:, None]
    packed_xT = pack_weight(n((K, T)) * s)
    return {
        "x_words": packed_xT[0],
        "x_scales": packed_xT[1],
        "hT": (n((K, V)) / np.sqrt(K) / s).astype(np.float32),
        "wgt": (np.tile(np.random.uniform(0.2, 1.5, T), (P, 1))).astype(np.float32),
        "isd0": (np.tile(np.random.uniform(0.1, 0.4, G), (P, 1))).astype(np.float32),
        "isd1": (np.tile(np.random.uniform(0.1, 0.4, G), (P, 1))).astype(np.float32),
        "isd2": (np.tile(np.random.uniform(0.1, 0.4, G), (P, 1))).astype(np.float32),
        "offs": striped(np.random.permutation(T)[:S]),
    }


def reference(x_words, x_scales, hT, wgt, isd0, isd1, isd2, offs):
    hTq = mxq(f64(hT), 0, "e4m3")
    xq = unpack_weight(x_words, x_scales)[:, unstriped(offs)]
    y = (hTq.T @ xq) * (f64(wgt)[:1][:, unstriped(offs)])
    y2 = (y) ** 2
    skat = y2.reshape(len(y2), -1, D).sum(axis=2)
    bur = (y.reshape(len(y), -1, D).sum(axis=2)) ** 2
    z0 = (0.9 * skat + 0.1 * bur - 8.0) * f64(isd0)[:1]
    z1 = (0.5 * skat + 0.5 * bur - 8.0) * f64(isd1)[:1]
    z2 = (0.1 * skat + 0.9 * bur - 8.0) * f64(isd2)[:1]
    return np.maximum(np.maximum(z0, z1), z2)

@@ -1,0 +1,193 @@
+from contextlib import ExitStack
+
+import concourse.mybir as mybir
+from concourse.masks import make_identity
+
+F32 = mybir.dt.float32
+BF16 = mybir.dt.bfloat16
+I32 = mybir.dt.int32
+U32 = mybir.dt.uint32
+U16 = mybir.dt.uint16
+U8 = mybir.dt.uint8
+FP8X4 = mybir.dt.float8_e4m3fn_x4
+ACT = mybir.ActivationFunctionType
+ALU = mybir.AluOpType
+AXIS = mybir.AxisListType
+
+P = 128
+PACK = 4
+K_PASS = P * PACK
+PASSES = 2
+VARIANTS = 1024
+PICKED = 512
+PHENOS = 512
+SETS = 64
+TILES = PICKED // P
+HALVES = 2
+HALF = PHENOS // HALVES
+BLOCKS = HALF // P
+MIXES = ((0.9, 0.1), (0.5, 0.5), (0.1, 0.9))
+OFFSET = 8.0
+VECTOR_CAST_COLUMNS = 176
+
+FLOPS = 2 * PASSES * K_PASS * PHENOS * PICKED
+
+
+def tile_picked_yskat_opt_p_kernel(
+    tc, x_words, x_scales, hT, wgt, isd0, isd1, isd2, offs, out
+):
+    nc = tc.nc
+    with ExitStack() as ctx:
+        keep = ctx.enter_context(tc.tile_pool(name="keep", bufs=1))
+        psum = ctx.enter_context(tc.psum_pool(name="psum", bufs=1))
+
+        offsets = keep.tile([P, PICKED // 16], U16, name="offsets")
+        nc.sync.dma_start(offsets[:], offs)
+
+        scale_window = keep.tile([P, VARIANTS], U8, name="scale_window", align_bytes=64)
+        nc.vector.memset(scale_window[:].bitcast(I32), 0)
+        weight_window = keep.tile([P, VARIANTS], F32, name="weight_window", align_bytes=64)
+        nc.vector.memset(weight_window[:], 0.0)
+
+        def load_words(o):
+            window = keep.tile([P, VARIANTS], U32, name="word_window%d" % o, align_bytes=64)
+            nc.sync.dma_start(
+                out=window[:].bitcast(I32), in_=x_words[o].rearrange("p n r -> p (n r)").bitcast(I32)
+            )
+            return window
+
+        word_windows = [load_words(0)]
+        for quadrant in range(4):
+            nc.sync.dma_start(
+                out=scale_window[32 * quadrant : 32 * quadrant + 4 * PASSES, :].bitcast(I32),
+                in_=x_scales[:, 4 * quadrant : 4 * quadrant + 4, :].bitcast(I32),
+            )
+        nc.sync.dma_start(out=weight_window[0:1, :], in_=wgt[0:1, :])
+        word_windows.append(load_words(1))
+
+        h_raw = {}
+        for half in range(HALVES):
+            for o in range(PASSES):
+                raw = keep.tile([P, PACK, HALF], F32, name="h_raw%d%d" % (half, o), align_bytes=64)
+                rows = hT[o * K_PASS : (o + 1) * K_PASS, half * HALF : (half + 1) * HALF]
+                nc.sync.dma_start(out=raw[:], in_=rows.rearrange("(p r) t -> p r t", r=PACK))
+                h_raw[half, o] = raw
+
+        identity = keep.tile([P, P], F32, name="identity")
+        make_identity(nc, identity[:])
+        isd = keep.tile([P, len(MIXES), SETS], F32, name="isd")
+        for m, rows in enumerate((isd0, isd1, isd2)):
+            nc.gpsimd.dma_start(out=isd[:, m, :], in_=rows)
+        gain = keep.tile([P, len(MIXES), SETS], F32, name="gain")
+        for m, (a, b) in enumerate(MIXES):
+            nc.gpsimd.tensor_scalar(gain[:, m, :], isd[:, m, :], a, 0.0, ALU.mult, ALU.add)
+
+        def gather(window, dtype, name):
+            picked = keep.tile([P, PICKED], dtype, name=name, align_bytes=64)
+            nc.vector.tensor_copy(picked[:].rearrange("p (i m) -> p m i", i=TILES), window[:].indirect(offsets[:]))
+            return picked
+
+        x_codes = [gather(word_windows[0], U32, "x_codes0")]
+        x_bytes = gather(scale_window, U8, "x_bytes")
+        x_codes.append(gather(word_windows[1], U32, "x_codes1"))
+
+        picked_weights = keep.tile([P, PICKED], F32, name="picked_weights", align_bytes=64)
+        nc.scalar.activation(picked_weights[:], weight_window[:].indirect(offsets[:]), ACT.Copy)
+        weight_bank = psum.tile([P, TILES, P], F32, name="weight_bank", tag="squares1")
+        for i in range(TILES):
+            nc.tensor.transpose(weight_bank[:, i, :], picked_weights[:, i::TILES], identity[:])
+        weights = keep.tile([P, TILES], F32, name="weights")
+        nc.scalar.copy(weights[:], weight_bank[:, :, 0])
+
+        def cast(engine_copy, grouped, raw, first, last):
+            engine_copy(
+                grouped[:, first:last, :].rearrange("p (c n) r -> p c r n", n=4),
+                raw[:, :, first:last].rearrange("p r (c n) -> p c r n", n=4),
+            )
+
+        h_codes, h_bytes = {}, {}
+        for half in range(HALVES):
+            for o in range(PASSES):
+                grouped = keep.tile([P, HALF, PACK], BF16, name="h_grouped%d%d" % (half, o), align_bytes=64)
+                split = VECTOR_CAST_COLUMNS if o == PASSES - 1 else 0
+                if split:
+                    cast(nc.vector.tensor_copy, grouped, h_raw[half, o], 0, split)
+                cast(nc.scalar.copy, grouped, h_raw[half, o], split, HALF)
+                codes = keep.tile([P, HALF], U32, name="h_codes%d%d" % (half, o), align_bytes=64)
+                plane = keep.tile([P, HALF], U8, name="h_bytes%d%d" % (half, o), align_bytes=64)
+                nc.vector.quantize_mx(
+                    out=codes[:].bitcast(FP8X4), scales=plane[:], in_=grouped[:].rearrange("p t r -> p (t r)")
+                )
+                h_codes[half, o], h_bytes[half, o] = codes, plane
+
+        for half in range(HALVES):
+            banks = [
+                psum.tile([P, 2, HALF], F32, name="scores%d%d" % (half, pair)) for pair in range(TILES // 2)
+            ]
+            for o in range(PASSES):
+                for i in range(TILES):
+                    columns = slice(i * P, (i + 1) * P)
+                    nc.tensor.matmul_mx(
+                        out=banks[i // 2][:, i % 2, :],
+                        lhsT=x_codes[o][:, columns].bitcast(FP8X4),
+                        lhsT_scale=x_bytes[4 * o : P, columns],
+                        rhs=h_codes[half, o][:].bitcast(FP8X4),
+                        rhs_scale=h_bytes[half, o][:],
+                        start=(o == 0 and i % 2 == 0),
+                        stop=(o == PASSES - 1 and i % 2 == 1),
+                    )
+
+            y = [keep.tile([P, 2, HALF], F32, name="y%d%d" % (half, pair)) for pair in range(TILES // 2)]
+            y2 = [keep.tile([P, 2, HALF], F32, name="y2%d%d" % (half, pair)) for pair in range(TILES // 2)]
+            nc.vector.tensor_tensor(
+                y[0][:], banks[0][:], weights[:, 0:2].unsqueeze(2).to_broadcast([P, 2, HALF]), ALU.mult
+            )
+            for i in (2, 3):
+                nc.scalar.activation(y[1][:, i - 2, :], banks[1][:, i - 2, :], ACT.Copy, scale=weights[:, i : i + 1])
+            for pair in range(TILES // 2):
+                nc.scalar.activation(y2[pair][:], y[pair][:], ACT.Square)
+
+            sums_bank = psum.tile([P, BLOCKS, P], F32, name="sums%d" % half, tag="sums%d" % half)
+            squares_bank = psum.tile([P, BLOCKS, P], F32, name="squares%d" % half, tag="squares%d" % half)
+            for bank, values in ((sums_bank, y), (squares_bank, y2)):
+                for block in range(BLOCKS):
+                    for i in range(TILES):
+                        nc.tensor.matmul(
+                            bank[:, block, :],
+                            values[i // 2][:, i % 2, block * P : (block + 1) * P],
+                            identity[:],
+                            start=(i == 0),
+                            stop=(i == TILES - 1),
+                            is_transpose=True,
+                        )
+
+            total = keep.tile([P, BLOCKS, SETS], F32, name="total%d" % half)
+            skat = keep.tile([P, BLOCKS, SETS], F32, name="skat%d" % half)
+            bur = keep.tile([P, BLOCKS, SETS], F32, name="bur%d" % half)
+            nc.vector.tensor_reduce(
+                total[:], sums_bank[:].rearrange("p b (g e) -> p b g e", e=2), AXIS.X, ALU.add
+            )
+            nc.scalar.activation(bur[:], total[:], ACT.Square)
+            nc.vector.tensor_reduce(
+                skat[:], squares_bank[:].rearrange("p b (g e) -> p b g e", e=2), AXIS.X, ALU.add
+            )
+            mixed = [keep.tile([P, BLOCKS, SETS], F32, name="mixed%d%d" % (half, m)) for m in range(len(MIXES))]
+            z = [keep.tile([P, BLOCKS, SETS], F32, name="z%d%d" % (half, m)) for m in range(len(MIXES))]
+            for m, (a, b) in enumerate(MIXES):
+                nc.vector.scalar_tensor_tensor(mixed[m][:], bur[:], b / a, skat[:], ALU.mult, ALU.add)
+            for m, (a, b) in enumerate(MIXES):
+                nc.vector.scalar_tensor_tensor(
+                    z[m][:],
+                    mixed[m][:],
+                    -OFFSET / a,
+                    gain[:, m, :].unsqueeze(1).to_broadcast([P, BLOCKS, SETS]),
+                    ALU.add,
+                    ALU.mult,
+                )
+            larger = keep.tile([P, BLOCKS, SETS], F32, name="larger%d" % half)
+            largest = keep.tile([P, BLOCKS, SETS], F32, name="largest%d" % half)
+            nc.vector.tensor_tensor(larger[:], z[0][:], z[1][:], ALU.max)
+            nc.vector.tensor_tensor(largest[:], larger[:], z[2][:], ALU.max)
+            nc.sync.dma_start(
+                out=out[half * HALF : (half + 1) * HALF, :].rearrange("(b p) g -> p b g", p=P), in_=largest[:]
+            )

@@ -1,3 +1,4 @@
+import math
 from contextlib import ExitStack
 
 import concourse.mybir as mybir
@@ -15,22 +16,30 @@ ALU = mybir.AluOpType
 AXIS = mybir.AxisListType
 
 P = 128
+QUADRANT = 32
 PACK = 4
 K_PASS = P * PACK
 PASSES = 2
 VARIANTS = 1024
 PICKED = 512
-PHENOS = 512
+PHENOTYPES = 512
 SETS = 64
 TILES = PICKED // P
-HALVES = 2
-HALF = PHENOS // HALVES
-BLOCKS = HALF // P
-MIXES = ((0.9, 0.1), (0.5, 0.5), (0.1, 0.9))
+BANK = 512
+MIXTURES = ((0.9, 0.1), (0.5, 0.5), (0.1, 0.9))
 OFFSET = 8.0
-VECTOR_CAST_COLUMNS = 176
 
-FLOPS = 2 * PASSES * K_PASS * PHENOS * PICKED
+UNITS = ((0, 256), (256, 128), (384, 128))
+CHUNKS = ((0, 0, 256, 192), (1, 0, 256, 128), (0, 256, 256, 128), (1, 256, 128, 128), (1, 384, 128, 128))
+SCORE_BANKS = (("a", "b"), ("c",), ("d",))
+SUM_BANKS = (("e", "f"), ("g", "h"), ("a", "b"))
+
+FLOPS = 2 * PASSES * K_PASS * PHENOTYPES * PICKED
+BYTES = (
+    PASSES * (K_PASS + K_PASS // 32) * VARIANTS
+    + 4 * (PASSES * K_PASS * PHENOTYPES + VARIANTS + len(MIXTURES) * P * SETS + PHENOTYPES * SETS)
+    + 2 * P * PICKED // 16
+)
 
 
 def tile_picked_yskat_opt_p_kernel(
@@ -41,153 +50,194 @@ def tile_picked_yskat_opt_p_kernel(
         keep = ctx.enter_context(tc.tile_pool(name="keep", bufs=1))
         psum = ctx.enter_context(tc.psum_pool(name="psum", bufs=1))
 
-        offsets = keep.tile([P, PICKED // 16], U16, name="offsets")
+        def sbuf(shape, dtype, name):
+            return keep.tile(shape, dtype, name=name, align_bytes=64)
+
+        offsets = sbuf([P, PICKED // 16], U16, "offsets")
         nc.sync.dma_start(offsets[:], offs)
 
-        scale_window = keep.tile([P, VARIANTS], U8, name="scale_window", align_bytes=64)
-        nc.vector.memset(scale_window[:].bitcast(I32), 0)
-        weight_window = keep.tile([P, VARIANTS], F32, name="weight_window", align_bytes=64)
-        nc.vector.memset(weight_window[:], 0.0)
+        scale_window = sbuf([P, VARIANTS], U8, "scale_window")
+        nc.gpsimd.memset(scale_window[:].bitcast(I32), 0)
+        weight_window = sbuf([P, VARIANTS], F32, "weight_window")
+        zero = sbuf([P, 1], F32, "zero")
+        nc.vector.memset(zero[:], 0.0)
+        last_quadrant = P - QUADRANT
+        nc.vector.memset(weight_window[0:last_quadrant, :], 0.0)
+        nc.scalar.activation(
+            weight_window[last_quadrant:P, :], zero[last_quadrant:P, :].to_broadcast([QUADRANT, VARIANTS]), ACT.Copy
+        )
 
         def load_words(o):
-            window = keep.tile([P, VARIANTS], U32, name="word_window%d" % o, align_bytes=64)
+            window = sbuf([P, VARIANTS], U32, "word_window%d" % o)
             nc.sync.dma_start(
                 out=window[:].bitcast(I32), in_=x_words[o].rearrange("p n r -> p (n r)").bitcast(I32)
             )
             return window
 
-        word_windows = [load_words(0)]
-        for quadrant in range(4):
+        def load_phenotypes(o, first, count):
+            raw = sbuf([P, PACK, count], F32, "h_raw%d_%d" % (o, first))
+            rows = hT[o * K_PASS : (o + 1) * K_PASS, first : first + count]
+            nc.sync.dma_start(out=raw[:], in_=rows.rearrange("(p r) t -> p r t", r=PACK))
+            return raw
+
+        for quadrant in range(P // QUADRANT):
             nc.sync.dma_start(
-                out=scale_window[32 * quadrant : 32 * quadrant + 4 * PASSES, :].bitcast(I32),
-                in_=x_scales[:, 4 * quadrant : 4 * quadrant + 4, :].bitcast(I32),
+                out=scale_window[QUADRANT * quadrant : QUADRANT * quadrant + PACK * PASSES, :].bitcast(I32),
+                in_=x_scales[:, PACK * quadrant : PACK * quadrant + PACK, :].bitcast(I32),
             )
+        word_windows = [load_words(0)]
         nc.sync.dma_start(out=weight_window[0:1, :], in_=wgt[0:1, :])
+        h_raw = [load_phenotypes(*CHUNKS[0][:3])]
         word_windows.append(load_words(1))
+        h_raw.extend(load_phenotypes(*chunk[:3]) for chunk in CHUNKS[1:])
 
-        h_raw = {}
-        for half in range(HALVES):
-            for o in range(PASSES):
-                raw = keep.tile([P, PACK, HALF], F32, name="h_raw%d%d" % (half, o), align_bytes=64)
-                rows = hT[o * K_PASS : (o + 1) * K_PASS, half * HALF : (half + 1) * HALF]
-                nc.sync.dma_start(out=raw[:], in_=rows.rearrange("(p r) t -> p r t", r=PACK))
-                h_raw[half, o] = raw
-
-        identity = keep.tile([P, P], F32, name="identity")
-        make_identity(nc, identity[:])
-        isd = keep.tile([P, len(MIXES), SETS], F32, name="isd")
+        isd = sbuf([P, len(MIXTURES), SETS], F32, "isd")
         for m, rows in enumerate((isd0, isd1, isd2)):
-            nc.gpsimd.dma_start(out=isd[:, m, :], in_=rows)
-        gain = keep.tile([P, len(MIXES), SETS], F32, name="gain")
-        for m, (a, b) in enumerate(MIXES):
-            nc.gpsimd.tensor_scalar(gain[:, m, :], isd[:, m, :], a, 0.0, ALU.mult, ALU.add)
+            nc.sync.dma_start(out=isd[:, m, :], in_=rows)
+        identity = sbuf([P, P], F32, "identity")
+        make_identity(nc, identity[:])
 
         def gather(window, dtype, name):
-            picked = keep.tile([P, PICKED], dtype, name=name, align_bytes=64)
+            picked = sbuf([P, PICKED], dtype, name)
             nc.vector.tensor_copy(picked[:].rearrange("p (i m) -> p m i", i=TILES), window[:].indirect(offsets[:]))
             return picked
 
-        x_codes = [gather(word_windows[0], U32, "x_codes0")]
         x_bytes = gather(scale_window, U8, "x_bytes")
-        x_codes.append(gather(word_windows[1], U32, "x_codes1"))
+        x_codes = [gather(word_windows[o], U32, "x_codes%d" % o) for o in range(PASSES)]
 
-        picked_weights = keep.tile([P, PICKED], F32, name="picked_weights", align_bytes=64)
+        picked_weights = sbuf([P, PICKED], F32, "picked_weights")
         nc.scalar.activation(picked_weights[:], weight_window[:].indirect(offsets[:]), ACT.Copy)
-        weight_bank = psum.tile([P, TILES, P], F32, name="weight_bank", tag="squares1")
+        weight_bank = psum.tile([P, TILES, P], F32, name="weight_bank", tag=SUM_BANKS[1][0])
         for i in range(TILES):
             nc.tensor.transpose(weight_bank[:, i, :], picked_weights[:, i::TILES], identity[:])
-        weights = keep.tile([P, TILES], F32, name="weights")
+        weights = sbuf([P, TILES], F32, "weights")
         nc.scalar.copy(weights[:], weight_bank[:, :, 0])
 
-        def cast(engine_copy, grouped, raw, first, last):
+        def round_columns(engine_copy, grouped, raw, first, last):
             engine_copy(
                 grouped[:, first:last, :].rearrange("p (c n) r -> p c r n", n=4),
                 raw[:, :, first:last].rearrange("p r (c n) -> p c r n", n=4),
             )
 
-        h_codes, h_bytes = {}, {}
-        for half in range(HALVES):
-            for o in range(PASSES):
-                grouped = keep.tile([P, HALF, PACK], BF16, name="h_grouped%d%d" % (half, o), align_bytes=64)
-                split = VECTOR_CAST_COLUMNS if o == PASSES - 1 else 0
-                if split:
-                    cast(nc.vector.tensor_copy, grouped, h_raw[half, o], 0, split)
-                cast(nc.scalar.copy, grouped, h_raw[half, o], split, HALF)
-                codes = keep.tile([P, HALF], U32, name="h_codes%d%d" % (half, o), align_bytes=64)
-                plane = keep.tile([P, HALF], U8, name="h_bytes%d%d" % (half, o), align_bytes=64)
-                nc.vector.quantize_mx(
-                    out=codes[:].bitcast(FP8X4), scales=plane[:], in_=grouped[:].rearrange("p t r -> p (t r)")
-                )
-                h_codes[half, o], h_bytes[half, o] = codes, plane
+        h_operand = {}
+        for raw, (o, first, count, on_vector) in zip(h_raw, CHUNKS):
+            grouped = sbuf([P, count, PACK], BF16, "h_grouped%d_%d" % (o, first))
+            round_columns(nc.vector.tensor_copy, grouped, raw, 0, on_vector)
+            if on_vector < count:
+                round_columns(nc.scalar.copy, grouped, raw, on_vector, count)
+            codes = sbuf([P, count], U32, "h_codes%d_%d" % (o, first))
+            scale_bytes = sbuf([P, count], U8, "h_bytes%d_%d" % (o, first))
+            nc.vector.quantize_mx(
+                out=codes[:].bitcast(FP8X4), scales=scale_bytes[:], in_=grouped[:].rearrange("p t r -> p (t r)")
+            )
+            for u, (start, size) in enumerate(UNITS):
+                if first <= start < first + count:
+                    columns = slice(start - first, start - first + size)
+                    h_operand[u, o] = (codes[:, columns], scale_bytes[:, columns])
 
-        for half in range(HALVES):
-            banks = [
-                psum.tile([P, 2, HALF], F32, name="scores%d%d" % (half, pair)) for pair in range(TILES // 2)
-            ]
+        scores = []
+        for u, (start, size) in enumerate(UNITS):
+            per_bank = BANK // size
+            banks = [psum.tile([P, per_bank, size], F32, name="scores_" + tag, tag=tag) for tag in SCORE_BANKS[u]]
             for o in range(PASSES):
                 for i in range(TILES):
                     columns = slice(i * P, (i + 1) * P)
                     nc.tensor.matmul_mx(
-                        out=banks[i // 2][:, i % 2, :],
+                        out=banks[i // per_bank][:, i % per_bank, :],
                         lhsT=x_codes[o][:, columns].bitcast(FP8X4),
-                        lhsT_scale=x_bytes[4 * o : P, columns],
-                        rhs=h_codes[half, o][:].bitcast(FP8X4),
-                        rhs_scale=h_bytes[half, o][:],
-                        start=(o == 0 and i % 2 == 0),
-                        stop=(o == PASSES - 1 and i % 2 == 1),
+                        lhsT_scale=x_bytes[PACK * o : P, columns],
+                        rhs=h_operand[u, o][0].bitcast(FP8X4),
+                        rhs_scale=h_operand[u, o][1],
+                        start=(o == 0 and i % per_bank == 0),
+                        stop=(o == PASSES - 1 and i % per_bank == per_bank - 1),
+                    )
+            scores.append([banks[i // per_bank][:, i % per_bank : i % per_bank + 2, :] for i in (0, 2)])
+
+        terms = []
+        for u, (start, size) in enumerate(UNITS):
+            low_scores, high_scores = scores[u]
+            low_y, pair_sums, low_squares, high_squares = (
+                sbuf([P, 2, size], F32, "%s%d" % (name, u))
+                for name in ("low_y", "pair_sums", "low_squares", "high_squares")
+            )
+
+            def square_high_tiles():
+                for j in range(2):
+                    nc.scalar.activation(
+                        high_squares[:, j, :], high_scores[:, j, :], ACT.Square, scale=weights[:, 2 + j : 3 + j]
                     )
 
-            y = [keep.tile([P, 2, HALF], F32, name="y%d%d" % (half, pair)) for pair in range(TILES // 2)]
-            y2 = [keep.tile([P, 2, HALF], F32, name="y2%d%d" % (half, pair)) for pair in range(TILES // 2)]
-            nc.vector.tensor_tensor(
-                y[0][:], banks[0][:], weights[:, 0:2].unsqueeze(2).to_broadcast([P, 2, HALF]), ALU.mult
+            if u == 0:
+                square_high_tiles()
+                for j in range(2):
+                    nc.scalar.activation(low_y[:, j, :], low_scores[:, j, :], ACT.Copy, scale=weights[:, j : j + 1])
+            else:
+                nc.vector.tensor_tensor(
+                    low_y[:], low_scores, weights[:, 0:2].unsqueeze(2).to_broadcast([P, 2, size]), ALU.mult
+                )
+            nc.scalar.activation(low_squares[:], low_y[:], ACT.Square)
+            for j in range(2):
+                nc.vector.scalar_tensor_tensor(
+                    pair_sums[:, j, :],
+                    high_scores[:, j, :],
+                    weights[:, 2 + j : 3 + j],
+                    low_y[:, j, :],
+                    ALU.mult,
+                    ALU.add,
+                )
+            if u > 0:
+                square_high_tiles()
+            terms.append(
+                (
+                    [pair_sums[:, j, :] for j in range(2)],
+                    [squares[:, j, :] for squares in (low_squares, high_squares) for j in range(2)],
+                )
             )
-            for i in (2, 3):
-                nc.scalar.activation(y[1][:, i - 2, :], banks[1][:, i - 2, :], ACT.Copy, scale=weights[:, i : i + 1])
-            for pair in range(TILES // 2):
-                nc.scalar.activation(y2[pair][:], y[pair][:], ACT.Square)
 
-            sums_bank = psum.tile([P, BLOCKS, P], F32, name="sums%d" % half, tag="sums%d" % half)
-            squares_bank = psum.tile([P, BLOCKS, P], F32, name="squares%d" % half, tag="squares%d" % half)
-            for bank, values in ((sums_bank, y), (squares_bank, y2)):
-                for block in range(BLOCKS):
-                    for i in range(TILES):
+        sums = []
+        for u, (start, size) in enumerate(UNITS):
+            unit_sums = []
+            for tag, addends in zip(SUM_BANKS[u], terms[u]):
+                bank = psum.tile([P, size // P, P], F32, name="sums%d_%s" % (u, tag), tag=tag)
+                for block in range(size // P):
+                    for n, addend in enumerate(addends):
                         nc.tensor.matmul(
                             bank[:, block, :],
-                            values[i // 2][:, i % 2, block * P : (block + 1) * P],
+                            addend[:, block * P : (block + 1) * P],
                             identity[:],
-                            start=(i == 0),
-                            stop=(i == TILES - 1),
+                            start=(n == 0),
+                            stop=(n == len(addends) - 1),
                             is_transpose=True,
                         )
+                unit_sums.append(bank[:].rearrange("p b (g e) -> p b g e", e=2))
+            sums.append(unit_sums)
 
-            total = keep.tile([P, BLOCKS, SETS], F32, name="total%d" % half)
-            skat = keep.tile([P, BLOCKS, SETS], F32, name="skat%d" % half)
-            bur = keep.tile([P, BLOCKS, SETS], F32, name="bur%d" % half)
-            nc.vector.tensor_reduce(
-                total[:], sums_bank[:].rearrange("p b (g e) -> p b g e", e=2), AXIS.X, ALU.add
+        for u, (start, size) in enumerate(UNITS):
+            blocks = size // P
+            total, skat, largest = (
+                sbuf([P, blocks, SETS], F32, "%s%d" % (name, u)) for name in ("total", "skat", "largest")
             )
-            nc.scalar.activation(bur[:], total[:], ACT.Square)
-            nc.vector.tensor_reduce(
-                skat[:], squares_bank[:].rearrange("p b (g e) -> p b g e", e=2), AXIS.X, ALU.add
+            burden, mixed, z = (
+                sbuf([P, blocks, len(MIXTURES), SETS], F32, "%s%d" % (name, u)) for name in ("burden", "mixed", "z")
             )
-            mixed = [keep.tile([P, BLOCKS, SETS], F32, name="mixed%d%d" % (half, m)) for m in range(len(MIXES))]
-            z = [keep.tile([P, BLOCKS, SETS], F32, name="z%d%d" % (half, m)) for m in range(len(MIXES))]
-            for m, (a, b) in enumerate(MIXES):
-                nc.vector.scalar_tensor_tensor(mixed[m][:], bur[:], b / a, skat[:], ALU.mult, ALU.add)
-            for m, (a, b) in enumerate(MIXES):
-                nc.vector.scalar_tensor_tensor(
-                    z[m][:],
-                    mixed[m][:],
-                    -OFFSET / a,
-                    gain[:, m, :].unsqueeze(1).to_broadcast([P, BLOCKS, SETS]),
-                    ALU.add,
-                    ALU.mult,
-                )
-            larger = keep.tile([P, BLOCKS, SETS], F32, name="larger%d" % half)
-            largest = keep.tile([P, BLOCKS, SETS], F32, name="largest%d" % half)
-            nc.vector.tensor_tensor(larger[:], z[0][:], z[1][:], ALU.max)
-            nc.vector.tensor_tensor(largest[:], larger[:], z[2][:], ALU.max)
-            nc.sync.dma_start(
-                out=out[half * HALF : (half + 1) * HALF, :].rearrange("(b p) g -> p b g", p=P), in_=largest[:]
+            nc.vector.tensor_reduce(total[:], sums[u][0], AXIS.X, ALU.add)
+            for m, (a, b) in enumerate(MIXTURES):
+                nc.scalar.activation(burden[:, :, m, :], total[:], ACT.Square, scale=math.sqrt(b))
+            nc.vector.tensor_reduce(skat[:], sums[u][1], AXIS.X, ALU.add)
+            for m, (a, b) in enumerate(MIXTURES):
+                nc.vector.scalar_tensor_tensor(mixed[:, :, m, :], skat[:], a, burden[:, :, m, :], ALU.mult, ALU.add)
+            nc.vector.scalar_tensor_tensor(
+                z[:].rearrange("p b m g -> p b (m g)"),
+                mixed[:].rearrange("p b m g -> p b (m g)"),
+                -OFFSET,
+                isd[:].rearrange("p m g -> p (m g)").unsqueeze(1).to_broadcast([P, blocks, len(MIXTURES) * SETS]),
+                ALU.add,
+                ALU.mult,
             )
+            if blocks > 1:
+                larger = sbuf([P, blocks, SETS], F32, "larger%d" % u)
+                nc.vector.tensor_tensor(larger[:], z[:, :, 0, :], z[:, :, 1, :], ALU.max)
+                nc.vector.tensor_tensor(largest[:], larger[:], z[:, :, 2, :], ALU.max)
+            else:
+                nc.vector.tensor_reduce(largest[:], z[:].rearrange("p b m g -> p b g m"), AXIS.X, ALU.max)
+            nc.sync.dma_start(out=out[start : start + size, :].rearrange("(b p) g -> p b g", p=P), in_=largest[:])

@@ -30,9 +30,10 @@ MIXTURES = ((0.9, 0.1), (0.5, 0.5), (0.1, 0.9))
 OFFSET = 8.0
 
 UNITS = ((0, 256), (256, 128), (384, 128))
-CHUNKS = ((0, 0, 256, 192), (1, 0, 256, 128), (0, 256, 256, 128), (1, 256, 128, 128), (1, 384, 128, 128))
+CHUNKS = ((0, 0, 256, 192), (1, 0, 256, 96), (0, 256, 256, 96), (1, 256, 128, 128), (1, 384, 128, 96))
 SCORE_BANKS = (("a", "b"), ("c",), ("d",))
 SUM_BANKS = (("e", "f"), ("g", "h"), ("a", "b"))
+LAST_STAGE = ((0,), (1, 2))
 
 FLOPS = 2 * PASSES * K_PASS * PHENOTYPES * PICKED
 BYTES = (
@@ -212,32 +213,44 @@ def tile_picked_yskat_opt_p_kernel(
                 unit_sums.append(bank[:].rearrange("p b (g e) -> p b g e", e=2))
             sums.append(unit_sums)
 
-        for u, (start, size) in enumerate(UNITS):
-            blocks = size // P
-            total, skat, largest = (
-                sbuf([P, blocks, SETS], F32, "%s%d" % (name, u)) for name in ("total", "skat", "largest")
-            )
-            burden, mixed, z = (
-                sbuf([P, blocks, len(MIXTURES), SETS], F32, "%s%d" % (name, u)) for name in ("burden", "mixed", "z")
-            )
-            nc.vector.tensor_reduce(total[:], sums[u][0], AXIS.X, ALU.add)
-            for m, (a, b) in enumerate(MIXTURES):
-                nc.scalar.activation(burden[:, :, m, :], total[:], ACT.Square, scale=math.sqrt(b))
-            nc.vector.tensor_reduce(skat[:], sums[u][1], AXIS.X, ALU.add)
-            for m, (a, b) in enumerate(MIXTURES):
-                nc.vector.scalar_tensor_tensor(mixed[:, :, m, :], skat[:], a, burden[:, :, m, :], ALU.mult, ALU.add)
-            nc.vector.scalar_tensor_tensor(
-                z[:].rearrange("p b m g -> p b (m g)"),
-                mixed[:].rearrange("p b m g -> p b (m g)"),
-                -OFFSET,
-                isd[:].rearrange("p m g -> p (m g)").unsqueeze(1).to_broadcast([P, blocks, len(MIXTURES) * SETS]),
-                ALU.add,
-                ALU.mult,
-            )
-            if blocks > 1:
-                larger = sbuf([P, blocks, SETS], F32, "larger%d" % u)
-                nc.vector.tensor_tensor(larger[:], z[:, :, 0, :], z[:, :, 1, :], ALU.max)
-                nc.vector.tensor_tensor(largest[:], larger[:], z[:, :, 2, :], ALU.max)
-            else:
-                nc.vector.tensor_reduce(largest[:], z[:].rearrange("p b m g -> p b g m"), AXIS.X, ALU.max)
-            nc.sync.dma_start(out=out[start : start + size, :].rearrange("(b p) g -> p b g", p=P), in_=largest[:])
+        blocks = [size // P for start, size in UNITS]
+        total, skat, largest = (
+            [sbuf([P, n, SETS], F32, "%s%d" % (name, u)) for u, n in enumerate(blocks)]
+            for name in ("total", "skat", "largest")
+        )
+        burden, mixed, z = (
+            [sbuf([P, n, len(MIXTURES), SETS], F32, "%s%d" % (name, u)) for u, n in enumerate(blocks)]
+            for name in ("burden", "mixed", "z")
+        )
+        isd_row = isd[:].rearrange("p m g -> p (m g)").unsqueeze(1)
+        for together in LAST_STAGE:
+            for u in together:
+                nc.vector.tensor_reduce(total[u][:], sums[u][0], AXIS.X, ALU.add)
+                for m, (a, b) in enumerate(MIXTURES):
+                    nc.scalar.activation(burden[u][:, :, m, :], total[u][:], ACT.Square, scale=math.sqrt(b))
+            for u in together:
+                nc.vector.tensor_reduce(skat[u][:], sums[u][1], AXIS.X, ALU.add)
+            for u in together:
+                for m, (a, b) in enumerate(MIXTURES):
+                    nc.vector.scalar_tensor_tensor(
+                        mixed[u][:, :, m, :], skat[u][:], a, burden[u][:, :, m, :], ALU.mult, ALU.add
+                    )
+            for u in together:
+                nc.vector.scalar_tensor_tensor(
+                    z[u][:].rearrange("p b m g -> p b (m g)"),
+                    mixed[u][:].rearrange("p b m g -> p b (m g)"),
+                    -OFFSET,
+                    isd_row.to_broadcast([P, blocks[u], len(MIXTURES) * SETS]),
+                    ALU.add,
+                    ALU.mult,
+                )
+            for u in together:
+                if blocks[u] > 1:
+                    larger = sbuf([P, blocks[u], SETS], F32, "larger%d" % u)
+                    nc.vector.tensor_tensor(larger[:], z[u][:, :, 0, :], z[u][:, :, 1, :], ALU.max)
+                    nc.vector.tensor_tensor(largest[u][:], larger[:], z[u][:, :, 2, :], ALU.max)
+                else:
+                    nc.vector.tensor_reduce(largest[u][:], z[u][:].rearrange("p b m g -> p b g m"), AXIS.X, ALU.max)
+                start, size = UNITS[u]
+                rows = out[start : start + size, :]
+                nc.sync.dma_start(out=rows.rearrange("(b p) g -> p b g", p=P), in_=largest[u][:])

@@ -30,7 +30,7 @@ MIXTURES = ((0.9, 0.1), (0.5, 0.5), (0.1, 0.9))
 OFFSET = 8.0
 
 UNITS = ((0, 256), (256, 128), (384, 128))
-CHUNKS = ((0, 0, 256, 192), (1, 0, 256, 96), (0, 256, 256, 96), (1, 256, 128, 128), (1, 384, 128, 96))
+CHUNKS = ((0, 0, 256, 64), (1, 0, 256, 64), (0, 256, 256, 96), (1, 256, 128, 128), (1, 384, 128, 96))
 SCORE_BANKS = (("a", "b"), ("c",), ("d",))
 SUM_BANKS = (("e", "f"), ("g", "h"), ("a", "b"))
 LAST_STAGE = ((0,), (1, 2))
@@ -81,12 +81,12 @@ def tile_picked_yskat_opt_p_kernel(
             nc.sync.dma_start(out=raw[:], in_=rows.rearrange("(p r) t -> p r t", r=PACK))
             return raw
 
+        word_windows = [load_words(0)]
         for quadrant in range(P // QUADRANT):
             nc.sync.dma_start(
                 out=scale_window[QUADRANT * quadrant : QUADRANT * quadrant + PACK * PASSES, :].bitcast(I32),
                 in_=x_scales[:, PACK * quadrant : PACK * quadrant + PACK, :].bitcast(I32),
             )
-        word_windows = [load_words(0)]
         nc.sync.dma_start(out=weight_window[0:1, :], in_=wgt[0:1, :])
         h_raw = [load_phenotypes(*CHUNKS[0][:3])]
         word_windows.append(load_words(1))
@@ -103,8 +103,9 @@ def tile_picked_yskat_opt_p_kernel(
             nc.vector.tensor_copy(picked[:].rearrange("p (i m) -> p m i", i=TILES), window[:].indirect(offsets[:]))
             return picked
 
+        x_codes = [gather(word_windows[0], U32, "x_codes0")]
         x_bytes = gather(scale_window, U8, "x_bytes")
-        x_codes = [gather(word_windows[o], U32, "x_codes%d" % o) for o in range(PASSES)]
+        x_codes.append(gather(word_windows[1], U32, "x_codes1"))
 
         picked_weights = sbuf([P, PICKED], F32, "picked_weights")
         nc.scalar.activation(picked_weights[:], weight_window[:].indirect(offsets[:]), ACT.Copy)

import math
from contextlib import ExitStack

import concourse.mybir as mybir
from concourse.masks import make_identity

F32 = mybir.dt.float32
BF16 = mybir.dt.bfloat16
I32 = mybir.dt.int32
U32 = mybir.dt.uint32
U16 = mybir.dt.uint16
U8 = mybir.dt.uint8
FP8X4 = mybir.dt.float8_e4m3fn_x4
ACT = mybir.ActivationFunctionType
ALU = mybir.AluOpType
AXIS = mybir.AxisListType

P = 128
QUADRANT = 32
PACK = 4
K_PASS = P * PACK
PASSES = 2
VARIANTS = 1024
PICKED = 512
PHENOTYPES = 512
SETS = 64
TILES = PICKED // P
BANK = 512
MIXTURES = ((0.9, 0.1), (0.5, 0.5), (0.1, 0.9))
OFFSET = 8.0

UNITS = ((0, 256), (256, 128), (384, 128))
CHUNKS = ((0, 0, 256, 64), (1, 0, 256, 64), (0, 256, 256, 96), (1, 256, 128, 128), (1, 384, 128, 96))
SCORE_BANKS = (("a", "b"), ("c",), ("d",))
SUM_BANKS = (("e", "f"), ("g", "h"), ("a", "b"))
LAST_STAGE = ((0,), (1, 2))

FLOPS = 2 * PASSES * K_PASS * PHENOTYPES * PICKED
BYTES = (
    PASSES * (K_PASS + K_PASS // 32) * VARIANTS
    + 4 * (PASSES * K_PASS * PHENOTYPES + VARIANTS + len(MIXTURES) * P * SETS + PHENOTYPES * SETS)
    + 2 * P * PICKED // 16
)


def tile_picked_yskat_opt_p_kernel(
    tc, x_words, x_scales, hT, wgt, isd0, isd1, isd2, offs, out
):
    nc = tc.nc
    with ExitStack() as ctx:
        keep = ctx.enter_context(tc.tile_pool(name="keep", bufs=1))
        psum = ctx.enter_context(tc.psum_pool(name="psum", bufs=1))

        def sbuf(shape, dtype, name):
            return keep.tile(shape, dtype, name=name, align_bytes=64)

        offsets = sbuf([P, PICKED // 16], U16, "offsets")
        nc.sync.dma_start(offsets[:], offs)

        scale_window = sbuf([P, VARIANTS], U8, "scale_window")
        nc.gpsimd.memset(scale_window[:].bitcast(I32), 0)
        weight_window = sbuf([P, VARIANTS], F32, "weight_window")
        zero = sbuf([P, 1], F32, "zero")
        nc.vector.memset(zero[:], 0.0)
        last_quadrant = P - QUADRANT
        nc.vector.memset(weight_window[0:last_quadrant, :], 0.0)
        nc.scalar.activation(
            weight_window[last_quadrant:P, :], zero[last_quadrant:P, :].to_broadcast([QUADRANT, VARIANTS]), ACT.Copy
        )

        def load_words(o):
            window = sbuf([P, VARIANTS], U32, "word_window%d" % o)
            nc.sync.dma_start(
                out=window[:].bitcast(I32), in_=x_words[o].rearrange("p n r -> p (n r)").bitcast(I32)
            )
            return window

        def load_phenotypes(o, first, count):
            raw = sbuf([P, PACK, count], F32, "h_raw%d_%d" % (o, first))
            rows = hT[o * K_PASS : (o + 1) * K_PASS, first : first + count]
            nc.sync.dma_start(out=raw[:], in_=rows.rearrange("(p r) t -> p r t", r=PACK))
            return raw

        word_windows = [load_words(0)]
        for quadrant in range(P // QUADRANT):
            nc.sync.dma_start(
                out=scale_window[QUADRANT * quadrant : QUADRANT * quadrant + PACK * PASSES, :].bitcast(I32),
                in_=x_scales[:, PACK * quadrant : PACK * quadrant + PACK, :].bitcast(I32),
            )
        nc.sync.dma_start(out=weight_window[0:1, :], in_=wgt[0:1, :])
        h_raw = [load_phenotypes(*CHUNKS[0][:3])]
        word_windows.append(load_words(1))
        h_raw.extend(load_phenotypes(*chunk[:3]) for chunk in CHUNKS[1:])

        isd = sbuf([P, len(MIXTURES), SETS], F32, "isd")
        for m, rows in enumerate((isd0, isd1, isd2)):
            nc.sync.dma_start(out=isd[:, m, :], in_=rows)
        identity = sbuf([P, P], F32, "identity")
        make_identity(nc, identity[:])

        def gather(window, dtype, name):
            picked = sbuf([P, PICKED], dtype, name)
            nc.vector.tensor_copy(picked[:].rearrange("p (i m) -> p m i", i=TILES), window[:].indirect(offsets[:]))
            return picked

        x_codes = [gather(word_windows[0], U32, "x_codes0")]
        x_bytes = gather(scale_window, U8, "x_bytes")
        x_codes.append(gather(word_windows[1], U32, "x_codes1"))

        picked_weights = sbuf([P, PICKED], F32, "picked_weights")
        nc.scalar.activation(picked_weights[:], weight_window[:].indirect(offsets[:]), ACT.Copy)
        weight_bank = psum.tile([P, TILES, P], F32, name="weight_bank", tag=SUM_BANKS[1][0])
        for i in range(TILES):
            nc.tensor.transpose(weight_bank[:, i, :], picked_weights[:, i::TILES], identity[:])
        weights = sbuf([P, TILES], F32, "weights")
        nc.scalar.copy(weights[:], weight_bank[:, :, 0])

        def round_columns(engine_copy, grouped, raw, first, last):
            engine_copy(
                grouped[:, first:last, :].rearrange("p (c n) r -> p c r n", n=4),
                raw[:, :, first:last].rearrange("p r (c n) -> p c r n", n=4),
            )

        h_operand = {}
        for raw, (o, first, count, on_vector) in zip(h_raw, CHUNKS):
            grouped = sbuf([P, count, PACK], BF16, "h_grouped%d_%d" % (o, first))
            round_columns(nc.vector.tensor_copy, grouped, raw, 0, on_vector)
            if on_vector < count:
                round_columns(nc.scalar.copy, grouped, raw, on_vector, count)
            codes = sbuf([P, count], U32, "h_codes%d_%d" % (o, first))
            scale_bytes = sbuf([P, count], U8, "h_bytes%d_%d" % (o, first))
            nc.vector.quantize_mx(
                out=codes[:].bitcast(FP8X4), scales=scale_bytes[:], in_=grouped[:].rearrange("p t r -> p (t r)")
            )
            for u, (start, size) in enumerate(UNITS):
                if first <= start < first + count:
                    columns = slice(start - first, start - first + size)
                    h_operand[u, o] = (codes[:, columns], scale_bytes[:, columns])

        scores = []
        for u, (start, size) in enumerate(UNITS):
            per_bank = BANK // size
            banks = [psum.tile([P, per_bank, size], F32, name="scores_" + tag, tag=tag) for tag in SCORE_BANKS[u]]
            for o in range(PASSES):
                for i in range(TILES):
                    columns = slice(i * P, (i + 1) * P)
                    nc.tensor.matmul_mx(
                        out=banks[i // per_bank][:, i % per_bank, :],
                        lhsT=x_codes[o][:, columns].bitcast(FP8X4),
                        lhsT_scale=x_bytes[PACK * o : P, columns],
                        rhs=h_operand[u, o][0].bitcast(FP8X4),
                        rhs_scale=h_operand[u, o][1],
                        start=(o == 0 and i % per_bank == 0),
                        stop=(o == PASSES - 1 and i % per_bank == per_bank - 1),
                    )
            scores.append([banks[i // per_bank][:, i % per_bank : i % per_bank + 2, :] for i in (0, 2)])

        terms = []
        for u, (start, size) in enumerate(UNITS):
            low_scores, high_scores = scores[u]
            low_y, pair_sums, low_squares, high_squares = (
                sbuf([P, 2, size], F32, "%s%d" % (name, u))
                for name in ("low_y", "pair_sums", "low_squares", "high_squares")
            )

            def square_high_tiles():
                for j in range(2):
                    nc.scalar.activation(
                        high_squares[:, j, :], high_scores[:, j, :], ACT.Square, scale=weights[:, 2 + j : 3 + j]
                    )

            if u == 0:
                square_high_tiles()
                for j in range(2):
                    nc.scalar.activation(low_y[:, j, :], low_scores[:, j, :], ACT.Copy, scale=weights[:, j : j + 1])
            else:
                nc.vector.tensor_tensor(
                    low_y[:], low_scores, weights[:, 0:2].unsqueeze(2).to_broadcast([P, 2, size]), ALU.mult
                )
            nc.scalar.activation(low_squares[:], low_y[:], ACT.Square)
            for j in range(2):
                nc.vector.scalar_tensor_tensor(
                    pair_sums[:, j, :],
                    high_scores[:, j, :],
                    weights[:, 2 + j : 3 + j],
                    low_y[:, j, :],
                    ALU.mult,
                    ALU.add,
                )
            if u > 0:
                square_high_tiles()
            terms.append(
                (
                    [pair_sums[:, j, :] for j in range(2)],
                    [squares[:, j, :] for squares in (low_squares, high_squares) for j in range(2)],
                )
            )

        sums = []
        for u, (start, size) in enumerate(UNITS):
            unit_sums = []
            for tag, addends in zip(SUM_BANKS[u], terms[u]):
                bank = psum.tile([P, size // P, P], F32, name="sums%d_%s" % (u, tag), tag=tag)
                for block in range(size // P):
                    for n, addend in enumerate(addends):
                        nc.tensor.matmul(
                            bank[:, block, :],
                            addend[:, block * P : (block + 1) * P],
                            identity[:],
                            start=(n == 0),
                            stop=(n == len(addends) - 1),
                            is_transpose=True,
                        )
                unit_sums.append(bank[:].rearrange("p b (g e) -> p b g e", e=2))
            sums.append(unit_sums)

        blocks = [size // P for start, size in UNITS]
        total, skat, largest = (
            [sbuf([P, n, SETS], F32, "%s%d" % (name, u)) for u, n in enumerate(blocks)]
            for name in ("total", "skat", "largest")
        )
        burden, mixed, z = (
            [sbuf([P, n, len(MIXTURES), SETS], F32, "%s%d" % (name, u)) for u, n in enumerate(blocks)]
            for name in ("burden", "mixed", "z")
        )
        isd_row = isd[:].rearrange("p m g -> p (m g)").unsqueeze(1)
        for together in LAST_STAGE:
            for u in together:
                nc.vector.tensor_reduce(total[u][:], sums[u][0], AXIS.X, ALU.add)
                for m, (a, b) in enumerate(MIXTURES):
                    nc.scalar.activation(burden[u][:, :, m, :], total[u][:], ACT.Square, scale=math.sqrt(b))
            for u in together:
                nc.vector.tensor_reduce(skat[u][:], sums[u][1], AXIS.X, ALU.add)
            for u in together:
                for m, (a, b) in enumerate(MIXTURES):
                    nc.vector.scalar_tensor_tensor(
                        mixed[u][:, :, m, :], skat[u][:], a, burden[u][:, :, m, :], ALU.mult, ALU.add
                    )
            for u in together:
                nc.vector.scalar_tensor_tensor(
                    z[u][:].rearrange("p b m g -> p b (m g)"),
                    mixed[u][:].rearrange("p b m g -> p b (m g)"),
                    -OFFSET,
                    isd_row.to_broadcast([P, blocks[u], len(MIXTURES) * SETS]),
                    ALU.add,
                    ALU.mult,
                )
            for u in together:
                if blocks[u] > 1:
                    larger = sbuf([P, blocks[u], SETS], F32, "larger%d" % u)
                    nc.vector.tensor_tensor(larger[:], z[u][:, :, 0, :], z[u][:, :, 1, :], ALU.max)
                    nc.vector.tensor_tensor(largest[u][:], larger[:], z[u][:, :, 2, :], ALU.max)
                else:
                    nc.vector.tensor_reduce(largest[u][:], z[u][:].rearrange("p b m g -> p b g m"), AXIS.X, ALU.max)
                start, size = UNITS[u]
                rows = out[start : start + size, :]
                nc.sync.dma_start(out=rows.rearrange("(b p) g -> p b g", p=P), in_=largest[u][:])
